import numpy as np
CORES = [13,21,141,149]
N = 4
F = 256
B1, B2, LR, EPS = 0.75, 0.875, 2.0, 0.001
def setup_inputs(rng):
    idle = rng.random((128, N * F)) < 0.125; ib = np.stack([idle[:, F * r:F * r + F] for r in range(N)])
    return {"gr": (rng.standard_normal((N, 128, N * F), dtype=np.float32) * ~idle), "m": (rng.standard_normal((N, 128, F), dtype=np.float32) * np.where(ib, 0.004, 1.0)).astype(np.float32), "v": np.where(ib, 2e-6 * 50 ** rng.random((N, 128, F)), (0.5 + rng.standard_normal((N, 128, F), dtype=np.float32) ** 2) * N).astype(np.float32), "w": rng.standard_normal((N, 128, F), dtype=np.float32)}
def setup_inputs_big(rng):
    d = setup_inputs(rng)
    for k in ("gr", "m", "v", "w"): d[k] = (d[k].astype(np.float32) * 1024.0).astype(d[k].dtype)
    return d
def setup_inputs_small(rng):
    d = setup_inputs(rng)
    for k in ("gr", "m", "v", "w"): d[k] = (d[k].astype(np.float32) * (1 / 1024.0)).astype(d[k].dtype)
    return d
def setup_inputs_apart(rng):
    d = setup_inputs(rng)
    f = (10.0 ** rng.permutation(np.linspace(-1.5, 1.5, N))).astype(np.float32).reshape(N, 1, 1)
    for k in ("gr", "m", "v", "w"): d[k] = (d[k].astype(np.float32) * f).astype(d[k].dtype)
    return d
def reference(gr, m, v, w):
    GR, M, V, W = gr.astype(np.float64), m.astype(np.float64), v.astype(np.float64), w.astype(np.float64)
    s = GR.sum(axis=0)
    sb = np.stack([s[:, F * r:F * r + F] for r in range(N)])
    m2 = B1 * M + (1 - B1) * sb
    v2 = B2 * V + (1 - B2) * sb ** 2
    w2 = W - LR * m2 / (np.sqrt(v2) + EPS)
    return {"y": np.broadcast_to(np.concatenate(list(w2), axis=1).astype(np.float32), (N, 128, N * F)), "mo": m2.astype(np.float32), "vo": v2.astype(np.float32)}

@@ -1,0 +1,226 @@
+from concourse.bass import DstId, RemoteDMATransfer
+from concourse.mybir import AluOpType, ActivationFunctionType
+
+N, F, K = 4, 256, 4
+W = F // K
+SIM_CORES = 256
+EPS = 0.001
+IN_X0, IN_X1, IN_P, IN_O, IN_V, IN_M, IN_W = range(7)
+
+_tile = ("sbuf", [128, W], "float32")
+_bank = ("psum", [128, 512], "float32")
+SCRATCH = {
+    "stage": ("dram", [7 * K, 128, W], "float32"),
+    "hin": ("dram", [7, 128, W], "float32"),
+    "yl": ("dram", [N * K, 128, W], "float32"),
+    "ml": ("dram", [K, 128, W], "float32"),
+    "vl": ("dram", [K, 128, W], "float32"),
+    "gO": _tile, "gP": _tile, "gXa": _tile, "gXb": _tile, "tv": _tile, "tm": _tile, "tw": _tile,
+    "v7": _tile, "s": _tile, "v8": _tile, "u": _tile, "vo_t": _tile, "mo_t": _tile, "wn": _tile,
+    "pA": _bank, "pB": _bank, "pC": _bank, "pD": _bank, "pE": _bank,
+}
+SEMAPHORES = ["ldx", "ldb", "ldc", "sent", "mi", "vi", "yin0", "yin1", "yin2", "yin3", "st",
+              "xin", "bin", "pin", "win", "lop", "lvm", "lw", "xa", "xb", "vq", "sq", "fwd"]
+
+
+def _bits(mask):
+    return [b for b in range(mask.bit_length()) if (mask >> b) & 1]
+
+
+def _mask(engines):
+    m = 0
+    for e in engines:
+        m |= 1 << e
+    return m
+
+
+def _take(pools, n, allowed):
+    out = []
+    for pool in pools:
+        for e in list(pool):
+            if len(out) < n and e in allowed:
+                pool.remove(e)
+                out.append(e)
+    return _mask(out)
+
+
+def _plan(T, topo):
+    cores = list(T.cores)
+    helpers, cross, plane = [], [], []
+    for i, rc in enumerate(cores):
+        own = [c for c in range(SIM_CORES)
+               if topo.host(c) == topo.host(rc) and topo.chip(c) == topo.chip(rc) and c != rc
+               and all(topo.may_write(c, d) for d in cores)]
+        own.sort(key=lambda c: (topo.die(c), c))
+        helpers.append(own[:K])
+        cross.append([k for k in range(N) if k != i and not topo.may_write(rc, cores[k])])
+        plane.append([k for k in range(N) if k != i and topo.may_write(rc, cores[k])])
+    return cores, helpers, cross, plane
+
+
+def _xfer(topo, src_core, dst_core, mask, sem, src, dst):
+    rid, pid = topo.addr(dst_core, src_core)
+    return RemoteDMATransfer(dst_ids=[DstId(rid=rid, pnc=pid)], dma_engine_mask=mask, remote_sem=sem, src=src, dst=dst)
+
+
+def _rank(g, core, T, topo, i, helpers, cross, plane):
+    S = T.sem
+    x0, x1 = cross[i]
+    p = plane[i][0]
+    mine = helpers[i]
+
+    def blk(s):
+        return T.stage[K * s:K * s + K]
+
+    def cols(r):
+        return T.gr[:, F * r:F * r + F]
+
+    g.sync.dma_start(blk(0), cols(x0)).then_inc(S.ldx, 16)
+    g.scalar.dma_start(blk(1), cols(x1)).then_inc(S.ldx, 16)
+    g.sync.dma_start(blk(2), cols(p)).then_inc(S.ldb, 16)
+    g.scalar.dma_start(blk(3), cols(i)).then_inc(S.ldb, 16)
+    g.sync.dma_start(blk(4), T.v[:]).then_inc(S.ldb, 16)
+    g.scalar.dma_start(blk(5), T.m[:]).then_inc(S.ldb, 16)
+    g.sync.dma_start(blk(6), T.w[:]).then_inc(S.ldc, 16)
+
+    on = _bits(topo.mask(core, mine[0]))
+    far = [topo.die(h) != topo.die(core) for h in mine]
+
+    def pools():
+        return list(on[0::2]), list(on[1::2])
+
+    ev, od = pools()
+    tr = []
+    for j, h in enumerate(mine):
+        pref = (ev, od) if far[j] else (od, ev)
+        for s, slot in ((0, IN_X0), (1, IN_X1)):
+            tr.append(_xfer(topo, core, h, _take(pref, 2, on), S.xin, T.stage[K * s + j], T.hin[slot]))
+    g.wait_ge(S.ldx, 32)
+    g.remote_dma_fused(tr, local_sem=S.sent)
+
+    ev, od = pools()
+    tr = []
+    for j, h in enumerate(helpers[p]):
+        tr.append(_xfer(topo, core, h, _take((ev, od), 1, _bits(topo.mask(core, h))), S.pin, T.stage[K * 2 + j], T.hin[IN_P]))
+    for want_far, items in ((True, ((3, IN_O), (4, IN_V))), (False, ((3, IN_O), (4, IN_V), (5, IN_M))), (True, ((5, IN_M),))):
+        for s, slot in items:
+            for j, h in enumerate(mine):
+                if far[j] == want_far:
+                    pref = (ev, od) if want_far else (od, ev)
+                    tr.append(_xfer(topo, core, h, _take(pref, 1, on), S.bin, T.stage[K * s + j], T.hin[slot]))
+    g.wait_ge(S.ldb, 64)
+    g.remote_dma_fused(tr, local_sem=S.sent)
+
+    ev, od = pools()
+    tr = []
+    for j, h in enumerate(mine):
+        pref = (ev, od) if far[j] else (od, ev)
+        tr.append(_xfer(topo, core, h, _take(pref, 4, on), S.win, T.stage[K * 6 + j], T.hin[IN_W]))
+    g.wait_ge(S.ldc, 16)
+    g.remote_dma_fused(tr, local_sem=S.sent)
+
+    def ystore(q, r):
+        q.wait_ge(S["yin%d" % r], 8 * K)
+        q.dma_start(T.y[:, F * r:F * r + F], T.yl[K * r:K * r + K]).then_inc(S.st, 16)
+
+    g.sync.wait_ge(S.mi, 4 * K)
+    g.sync.dma_start(T.mo[:], T.ml[0:K]).then_inc(S.st, 16)
+    g.scalar.wait_ge(S.vi, 4 * K)
+    g.scalar.dma_start(T.vo[:], T.vl[0:K]).then_inc(S.st, 16)
+    ystore(g.sync, i)
+    ystore(g.scalar, p)
+    ystore(g.sync, x0)
+    ystore(g.scalar, x1)
+    g.wait_ge(S.sent, 48)
+    g.wait_ge(S.st, 96)
+
+
+def _helper(g, core, T, topo, i, j, cores, helpers, cross, plane):
+    S = T.sem
+    v = g.vector
+    A = AluOpType
+    rc = cores[i]
+
+    tr = []
+    for n, k in enumerate(cross[i]):
+        dst = helpers[k][j]
+        off = _bits(topo.mask(core, dst))
+        half = len(off) // 2
+        first = cross[k].index(i) == 0
+        tr.append(_xfer(topo, core, dst, _mask(off[n * half:(n + 1) * half]), S.xa if first else S.xb,
+                        T.hin[(IN_X0, IN_X1)[n]], (T.gXa if first else T.gXb)[:]))
+    g.wait_ge(S.xin, 4)
+    g.remote_dma_fused(tr, local_sem=S.fwd)
+
+    g.sync.wait_ge(S.bin, 3)
+    g.sync.dma_start(T.gO[:], T.hin[IN_O]).then_inc(S.lop, 16)
+    g.sync.dma_start(T.tv[:], T.hin[IN_V]).then_inc(S.lvm, 16)
+    g.sync.dma_start(T.tm[:], T.hin[IN_M]).then_inc(S.lvm, 16)
+    g.sync.wait_ge(S.win, 4)
+    g.sync.dma_start(T.tw[:], T.hin[IN_W]).then_inc(S.lw, 16)
+    g.scalar.wait_ge(S.pin, 1)
+    g.scalar.dma_start(T.gP[:], T.hin[IN_P]).then_inc(S.lop, 16)
+
+    pA, pB, pC, pD, pE = (T[n][:, 0:W] for n in ("pA", "pB", "pC", "pD", "pE"))
+    done = [0]
+
+    def vop(ins):
+        ins.then_inc(S.vq, 1)
+        done[0] += 1
+        v.wait_ge(S.vq, done[0])
+
+    v.wait_ge(S.lvm, 32)
+    vop(v.tensor_scalar(T.v7[:], T.tv[:], 7.0, None, A.mult))
+    vop(v.tensor_scalar(pE, T.tm[:], 3.0, None, A.mult))
+    v.wait_ge(S.lop, 32)
+    vop(v.tensor_tensor(pA, T.gO[:], T.gP[:], A.add))
+    v.wait_ge(S.xa, 4)
+    vop(v.tensor_tensor(pB, pA, T.gXa[:], A.add))
+    v.wait_ge(S.xb, 4)
+    vop(v.tensor_tensor(T.s[:], pB, T.gXb[:], A.add))
+    vop(v.tensor_tensor(pC, T.s[:], T.s[:], A.mult))
+    vop(v.tensor_tensor(T.v8[:], pC, T.v7[:], A.add))
+    g.scalar.wait_ge(S.vq, done[0])
+    g.scalar.activation(pD, T.v8[:], ActivationFunctionType.Sqrt, scale=0.5).then_inc(S.sq, 1)
+    vop(v.tensor_scalar(T.vo_t[:], T.v8[:], 0.125, None, A.mult))
+    vop(v.tensor_tensor(T.u[:], pE, T.s[:], A.add))
+    vop(v.tensor_scalar(T.mo_t[:], T.u[:], 0.25, None, A.mult))
+    mv_ready = done[0]
+    v.wait_ge(S.sq, 1)
+    vop(v.tensor_scalar(pD, pD, 2.0 * EPS, None, A.add))
+    vop(v.reciprocal(pD, pD))
+    vop(v.tensor_tensor(pC, T.u[:], pD, A.mult))
+    v.wait_ge(S.lw, 16)
+    vop(v.tensor_tensor(T.wn[:], T.tw[:], pC, A.subtract))
+    w_ready = done[0]
+
+    peers = [cores[k] for k in cross[i] + plane[i]]
+    off = _bits(topo.mask(core, peers[0]))
+    for d in peers:
+        off = [e for e in off if e in _bits(topo.mask(core, d))]
+    rest = [e for e in _bits(topo.mask(core, rc)) if e not in off]
+    half = len(rest) // 2
+    g.wait_ge(S.vq, mv_ready)
+    g.remote_dma_fused([_xfer(topo, core, rc, _mask(rest[:half]), S.mi, T.mo_t[:], T.ml[j]),
+                        _xfer(topo, core, rc, _mask(rest[half:]), S.vi, T.vo_t[:], T.vl[j])], local_sem=S.fwd)
+    ysem = S["yin%d" % i]
+    ids = []
+    for d in peers:
+        rid, pid = topo.addr(d, core)
+        ids.append(DstId(rid=rid, pnc=pid))
+    g.wait_ge(S.vq, w_ready)
+    g.remote_dma_fused([RemoteDMATransfer(dst_ids=ids, dma_engine_mask=_mask(off), remote_sem=ysem, srcs=[T.wn[:]],
+                                          dsts=[T.yl[K * i + j] for _ in peers]),
+                        _xfer(topo, core, rc, _mask(rest), ysem, T.wn[:], T.yl[K * i + j])], local_sem=S.fwd)
+    g.wait_ge(S.fwd, 2 * len(off) + 2 * len(rest))
+
+
+def rank_program(g, core, T, topo):
+    cores, helpers, cross, plane = _plan(T, topo)
+    rank = T.rank_of(core)
+    if rank is not None:
+        _rank(g, core, T, topo, rank, helpers, cross, plane)
+        return
+    for i in range(N):
+        if core in helpers[i]:
+            _helper(g, core, T, topo, i, helpers[i].index(core), cores, helpers, cross, plane)

@@ -5,7 +5,7 @@ N, F, K = 4, 256, 4
 W = F // K
 SIM_CORES = 256
 EPS = 0.001
-IN_X0, IN_X1, IN_P, IN_O, IN_V, IN_M, IN_W = range(7)
+X0, X1, P, O, V, M, WW = range(7)
 
 _tile = ("sbuf", [128, W], "float32")
 _bank = ("psum", [128, 512], "float32")
@@ -19,8 +19,8 @@ SCRATCH = {
     "v7": _tile, "s": _tile, "v8": _tile, "u": _tile, "vo_t": _tile, "mo_t": _tile, "wn": _tile,
     "pA": _bank, "pB": _bank, "pC": _bank, "pD": _bank, "pE": _bank,
 }
-SEMAPHORES = ["ldx", "ldb", "ldc", "sent", "mi", "vi", "yin0", "yin1", "yin2", "yin3", "st",
-              "xin", "bin", "pin", "win", "lop", "lvm", "lw", "xa", "xb", "vq", "sq", "fwd"]
+SEMAPHORES = ["ld1", "ld2", "ld3", "ld4", "sent", "mi", "vi", "yin0", "yin1", "yin2", "yin3", "st",
+              "xin0", "xin1", "pin", "ovin", "mwin", "lop", "lv", "lm", "lw", "xa", "xb", "vq", "sq", "fwd"]
 
 
 def _bits(mask):
@@ -34,16 +34,6 @@ def _mask(engines):
     return m
 
 
-def _take(pools, n, allowed):
-    out = []
-    for pool in pools:
-        for e in list(pool):
-            if len(out) < n and e in allowed:
-                pool.remove(e)
-                out.append(e)
-    return _mask(out)
-
-
 def _plan(T, topo):
     cores = list(T.cores)
     helpers, cross, plane = [], [], []
@@ -53,8 +43,9 @@ def _plan(T, topo):
                and all(topo.may_write(c, d) for d in cores)]
         own.sort(key=lambda c: (topo.die(c), c))
         helpers.append(own[:K])
-        cross.append([k for k in range(N) if k != i and not topo.may_write(rc, cores[k])])
-        plane.append([k for k in range(N) if k != i and topo.may_write(rc, cores[k])])
+        around = [(i + d) % N for d in range(1, N)]
+        cross.append([k for k in around if not topo.may_write(rc, cores[k])])
+        plane.append([k for k in around if topo.may_write(rc, cores[k])])
     return cores, helpers, cross, plane
 
 
@@ -69,69 +60,63 @@ def _rank(g, core, T, topo, i, helpers, cross, plane):
     p = plane[i][0]
     mine = helpers[i]
 
-    def blk(s):
-        return T.stage[K * s:K * s + K]
+    def load(q, s, src, sem):
+        q.dma_start(T.stage[K * s:K * s + K], src).then_inc(sem, 16)
 
     def cols(r):
         return T.gr[:, F * r:F * r + F]
 
-    g.sync.dma_start(blk(0), cols(x0)).then_inc(S.ldx, 16)
-    g.scalar.dma_start(blk(1), cols(x1)).then_inc(S.ldx, 16)
-    g.sync.dma_start(blk(2), cols(p)).then_inc(S.ldb, 16)
-    g.scalar.dma_start(blk(3), cols(i)).then_inc(S.ldb, 16)
-    g.sync.dma_start(blk(4), T.v[:]).then_inc(S.ldb, 16)
-    g.scalar.dma_start(blk(5), T.m[:]).then_inc(S.ldb, 16)
-    g.sync.dma_start(blk(6), T.w[:]).then_inc(S.ldc, 16)
+    load(g.sync, X0, cols(x0), S.ld1)
+    load(g.scalar, X1, cols(x1), S.ld2)
+    load(g.sync, P, cols(p), S.ld2)
+    load(g.scalar, O, cols(i), S.ld3)
+    load(g.sync, V, T.v[:], S.ld3)
+    load(g.scalar, M, T.m[:], S.ld4)
+    load(g.sync, WW, T.w[:], S.ld4)
 
     on = _bits(topo.mask(core, mine[0]))
+    off = _bits(topo.mask(core, helpers[p][0]))
     far = [topo.die(h) != topo.die(core) for h in mine]
 
-    def pools():
-        return list(on[0::2]), list(on[1::2])
-
-    ev, od = pools()
-    tr = []
-    for j, h in enumerate(mine):
-        pref = (ev, od) if far[j] else (od, ev)
-        for s, slot in ((0, IN_X0), (1, IN_X1)):
-            tr.append(_xfer(topo, core, h, _take(pref, 2, on), S.xin, T.stage[K * s + j], T.hin[slot]))
-    g.wait_ge(S.ldx, 32)
-    g.remote_dma_fused(tr, local_sem=S.sent)
-
-    ev, od = pools()
-    tr = []
-    for j, h in enumerate(helpers[p]):
-        tr.append(_xfer(topo, core, h, _take((ev, od), 1, _bits(topo.mask(core, h))), S.pin, T.stage[K * 2 + j], T.hin[IN_P]))
-    for want_far, items in ((True, ((3, IN_O), (4, IN_V))), (False, ((3, IN_O), (4, IN_V), (5, IN_M))), (True, ((5, IN_M),))):
-        for s, slot in items:
+    def to_helpers(items, engines):
+        n = len(engines) // (K * len(items))
+        pool = {True: list(engines[0::2]), False: list(engines[1::2])}
+        tr = []
+        for s, sem in items:
             for j, h in enumerate(mine):
-                if far[j] == want_far:
-                    pref = (ev, od) if want_far else (od, ev)
-                    tr.append(_xfer(topo, core, h, _take(pref, 1, on), S.bin, T.stage[K * s + j], T.hin[slot]))
-    g.wait_ge(S.ldb, 64)
+                e = [pool[far[j]].pop(0) for _ in range(n)]
+                tr.append(_xfer(topo, core, h, _mask(e), sem, T.stage[K * s + j], T.hin[s]))
+        return tr
+
+    g.wait_ge(S.ld1, 16)
+    g.remote_dma_fused(to_helpers([(X0, S.xin0)], on), local_sem=S.sent)
+
+    n = len(off) // K
+    tr = [_xfer(topo, core, h, _mask(off[n * j:n * j + n]), S.pin, T.stage[K * P + j], T.hin[P])
+          for j, h in enumerate(helpers[p])]
+    tr += to_helpers([(X1, S.xin1)], [e for e in on if e not in off])
+    g.wait_ge(S.ld2, 32)
     g.remote_dma_fused(tr, local_sem=S.sent)
 
-    ev, od = pools()
-    tr = []
-    for j, h in enumerate(mine):
-        pref = (ev, od) if far[j] else (od, ev)
-        tr.append(_xfer(topo, core, h, _take(pref, 4, on), S.win, T.stage[K * 6 + j], T.hin[IN_W]))
-    g.wait_ge(S.ldc, 16)
-    g.remote_dma_fused(tr, local_sem=S.sent)
+    g.wait_ge(S.ld3, 32)
+    g.remote_dma_fused(to_helpers([(O, S.ovin), (V, S.ovin)], on), local_sem=S.sent)
+    g.wait_ge(S.ld4, 32)
+    g.remote_dma_fused(to_helpers([(M, S.mwin), (WW, S.mwin)], on), local_sem=S.sent)
 
     def ystore(q, r):
         q.wait_ge(S["yin%d" % r], 8 * K)
         q.dma_start(T.y[:, F * r:F * r + F], T.yl[K * r:K * r + K]).then_inc(S.st, 16)
 
+    first, second, third = sorted((x0, x1, p), key=lambda k: (cross[k] + plane[k]).index(i))
     g.sync.wait_ge(S.mi, 4 * K)
     g.sync.dma_start(T.mo[:], T.ml[0:K]).then_inc(S.st, 16)
     g.scalar.wait_ge(S.vi, 4 * K)
     g.scalar.dma_start(T.vo[:], T.vl[0:K]).then_inc(S.st, 16)
-    ystore(g.sync, i)
-    ystore(g.scalar, p)
-    ystore(g.sync, x0)
-    ystore(g.scalar, x1)
-    g.wait_ge(S.sent, 48)
+    ystore(g.scalar, i)
+    ystore(g.sync, first)
+    ystore(g.scalar, second)
+    ystore(g.sync, third)
+    g.wait_ge(S.sent, 4 * len(on))
     g.wait_ge(S.st, 96)
 
 
@@ -140,49 +125,51 @@ def _helper(g, core, T, topo, i, j, cores, helpers, cross, plane):
     v = g.vector
     A = AluOpType
     rc = cores[i]
+    n_on = len(_bits(topo.mask(rc, core)))
+    n_out = len(_bits(topo.mask(cores[plane[i][0]], core)))
 
-    tr = []
+    n_off = 0
     for n, k in enumerate(cross[i]):
         dst = helpers[k][j]
-        off = _bits(topo.mask(core, dst))
-        half = len(off) // 2
-        first = cross[k].index(i) == 0
-        tr.append(_xfer(topo, core, dst, _mask(off[n * half:(n + 1) * half]), S.xa if first else S.xb,
-                        T.hin[(IN_X0, IN_X1)[n]], (T.gXa if first else T.gXb)[:]))
-    g.wait_ge(S.xin, 4)
-    g.remote_dma_fused(tr, local_sem=S.fwd)
+        rid, pid = topo.addr(dst, core)
+        m = topo.mask(core, dst)
+        n_off = len(_bits(m))
+        g.wait_ge((S.xin0, S.xin1)[n], (n_on // K, (n_on - n_out) // K)[n])
+        g.remote_dma((T.gXa, T.gXb)[n][:], T.hin[(X0, X1)[n]], (S.xa, S.xb)[n], S.fwd, pid, rid, m)
 
-    g.sync.wait_ge(S.bin, 3)
-    g.sync.dma_start(T.gO[:], T.hin[IN_O]).then_inc(S.lop, 16)
-    g.sync.dma_start(T.tv[:], T.hin[IN_V]).then_inc(S.lvm, 16)
-    g.sync.dma_start(T.tm[:], T.hin[IN_M]).then_inc(S.lvm, 16)
-    g.sync.wait_ge(S.win, 4)
-    g.sync.dma_start(T.tw[:], T.hin[IN_W]).then_inc(S.lw, 16)
-    g.scalar.wait_ge(S.pin, 1)
-    g.scalar.dma_start(T.gP[:], T.hin[IN_P]).then_inc(S.lop, 16)
+    g.scalar.wait_ge(S.pin, n_out // K)
+    g.scalar.dma_start(T.gP[:], T.hin[P]).then_inc(S.lop, 16)
+    g.sync.wait_ge(S.ovin, n_on // K)
+    g.sync.dma_start(T.gO[:], T.hin[O]).then_inc(S.lop, 16)
+    g.sync.dma_start(T.tv[:], T.hin[V]).then_inc(S.lv, 16)
+    g.sync.wait_ge(S.mwin, n_on // K)
+    g.sync.dma_start(T.tm[:], T.hin[M]).then_inc(S.lm, 16)
+    g.sync.dma_start(T.tw[:], T.hin[WW]).then_inc(S.lw, 16)
 
     pA, pB, pC, pD, pE = (T[n][:, 0:W] for n in ("pA", "pB", "pC", "pD", "pE"))
     done = [0]
 
-    def vop(ins):
+    def vop(ins, wait=True):
         ins.then_inc(S.vq, 1)
         done[0] += 1
-        v.wait_ge(S.vq, done[0])
+        if wait:
+            v.wait_ge(S.vq, done[0])
 
-    v.wait_ge(S.lvm, 32)
-    vop(v.tensor_scalar(T.v7[:], T.tv[:], 7.0, None, A.mult))
-    vop(v.tensor_scalar(pE, T.tm[:], 3.0, None, A.mult))
+    v.wait_ge(S.lv, 16)
+    vop(v.tensor_scalar(T.v7[:], T.tv[:], 7.0, None, A.mult), wait=False)
     v.wait_ge(S.lop, 32)
     vop(v.tensor_tensor(pA, T.gO[:], T.gP[:], A.add))
-    v.wait_ge(S.xa, 4)
+    v.wait_ge(S.xa, n_off)
     vop(v.tensor_tensor(pB, pA, T.gXa[:], A.add))
-    v.wait_ge(S.xb, 4)
+    v.wait_ge(S.xb, n_off)
     vop(v.tensor_tensor(T.s[:], pB, T.gXb[:], A.add))
     vop(v.tensor_tensor(pC, T.s[:], T.s[:], A.mult))
     vop(v.tensor_tensor(T.v8[:], pC, T.v7[:], A.add))
     g.scalar.wait_ge(S.vq, done[0])
     g.scalar.activation(pD, T.v8[:], ActivationFunctionType.Sqrt, scale=0.5).then_inc(S.sq, 1)
-    vop(v.tensor_scalar(T.vo_t[:], T.v8[:], 0.125, None, A.mult))
+    vop(v.tensor_scalar(T.vo_t[:], T.v8[:], 0.125, None, A.mult), wait=False)
+    v.wait_ge(S.lm, 16)
+    vop(v.tensor_scalar(pE, T.tm[:], 3.0, None, A.mult))
     vop(v.tensor_tensor(T.u[:], pE, T.s[:], A.add))
     vop(v.tensor_scalar(T.mo_t[:], T.u[:], 0.25, None, A.mult))
     mv_ready = done[0]
@@ -200,6 +187,7 @@ def _helper(g, core, T, topo, i, j, cores, helpers, cross, plane):
         off = [e for e in off if e in _bits(topo.mask(core, d))]
     rest = [e for e in _bits(topo.mask(core, rc)) if e not in off]
     half = len(rest) // 2
+
     g.wait_ge(S.vq, mv_ready)
     g.remote_dma_fused([_xfer(topo, core, rc, _mask(rest[:half]), S.mi, T.mo_t[:], T.ml[j]),
                         _xfer(topo, core, rc, _mask(rest[half:]), S.vi, T.vo_t[:], T.vl[j])], local_sem=S.fwd)
@@ -212,7 +200,7 @@ def _helper(g, core, T, topo, i, j, cores, helpers, cross, plane):
     g.remote_dma_fused([RemoteDMATransfer(dst_ids=ids, dma_engine_mask=_mask(off), remote_sem=ysem, srcs=[T.wn[:]],
                                           dsts=[T.yl[K * i + j] for _ in peers]),
                         _xfer(topo, core, rc, _mask(rest), ysem, T.wn[:], T.yl[K * i + j])], local_sem=S.fwd)
-    g.wait_ge(S.fwd, 2 * len(off) + 2 * len(rest))
+    g.wait_ge(S.fwd, 2 * n_off + len(off) + 2 * len(rest))
 
 
 def rank_program(g, core, T, topo):

from concourse.bass import DstId, RemoteDMATransfer
from concourse.mybir import AluOpType, ActivationFunctionType

N, F, K = 4, 256, 4
W = F // K
SIM_CORES = 256
EPS = 0.001
X0, X1, P, O, V, M, WW = range(7)

_tile = ("sbuf", [128, W], "float32")
_bank = ("psum", [128, 512], "float32")
SCRATCH = {
    "stage": ("dram", [7 * K, 128, W], "float32"),
    "hin": ("dram", [7, 128, W], "float32"),
    "yl": ("dram", [N * K, 128, W], "float32"),
    "ml": ("dram", [K, 128, W], "float32"),
    "vl": ("dram", [K, 128, W], "float32"),
    "gO": _tile, "gP": _tile, "gXa": _tile, "gXb": _tile, "tv": _tile, "tm": _tile, "tw": _tile,
    "v7": _tile, "s": _tile, "v8": _tile, "u": _tile, "vo_t": _tile, "mo_t": _tile, "wn": _tile,
    "pA": _bank, "pB": _bank, "pC": _bank, "pD": _bank, "pE": _bank,
}
SEMAPHORES = ["ld1", "ld2", "ld3", "ld4", "sent", "mi", "vi", "yin0", "yin1", "yin2", "yin3", "st",
              "xin0", "xin1", "pin", "ovin", "mwin", "lop", "lv", "lm", "lw", "xa", "xb", "vq", "sq", "fwd"]


def _bits(mask):
    return [b for b in range(mask.bit_length()) if (mask >> b) & 1]


def _mask(engines):
    m = 0
    for e in engines:
        m |= 1 << e
    return m


def _plan(T, topo):
    cores = list(T.cores)
    helpers, cross, plane = [], [], []
    for i, rc in enumerate(cores):
        own = [c for c in range(SIM_CORES)
               if topo.host(c) == topo.host(rc) and topo.chip(c) == topo.chip(rc) and c != rc
               and all(topo.may_write(c, d) for d in cores)]
        own.sort(key=lambda c: (topo.die(c), c))
        helpers.append(own[:K])
        around = [(i + d) % N for d in range(1, N)]
        cross.append([k for k in around if not topo.may_write(rc, cores[k])])
        plane.append([k for k in around if topo.may_write(rc, cores[k])])
    return cores, helpers, cross, plane


def _xfer(topo, src_core, dst_core, mask, sem, src, dst):
    rid, pid = topo.addr(dst_core, src_core)
    return RemoteDMATransfer(dst_ids=[DstId(rid=rid, pnc=pid)], dma_engine_mask=mask, remote_sem=sem, src=src, dst=dst)


def _rank(g, core, T, topo, i, helpers, cross, plane):
    S = T.sem
    x0, x1 = cross[i]
    p = plane[i][0]
    mine = helpers[i]

    def load(q, s, src, sem):
        q.dma_start(T.stage[K * s:K * s + K], src).then_inc(sem, 16)

    def cols(r):
        return T.gr[:, F * r:F * r + F]

    load(g.sync, X0, cols(x0), S.ld1)
    load(g.scalar, X1, cols(x1), S.ld2)
    load(g.sync, P, cols(p), S.ld2)
    load(g.scalar, O, cols(i), S.ld3)
    load(g.sync, V, T.v[:], S.ld3)
    load(g.scalar, M, T.m[:], S.ld4)
    load(g.sync, WW, T.w[:], S.ld4)

    on = _bits(topo.mask(core, mine[0]))
    off = _bits(topo.mask(core, helpers[p][0]))
    far = [topo.die(h) != topo.die(core) for h in mine]

    def to_helpers(items, engines):
        n = len(engines) // (K * len(items))
        pool = {True: list(engines[0::2]), False: list(engines[1::2])}
        tr = []
        for s, sem in items:
            for j, h in enumerate(mine):
                e = [pool[far[j]].pop(0) for _ in range(n)]
                tr.append(_xfer(topo, core, h, _mask(e), sem, T.stage[K * s + j], T.hin[s]))
        return tr

    g.wait_ge(S.ld1, 16)
    g.remote_dma_fused(to_helpers([(X0, S.xin0)], on), local_sem=S.sent)

    n = len(off) // K
    tr = [_xfer(topo, core, h, _mask(off[n * j:n * j + n]), S.pin, T.stage[K * P + j], T.hin[P])
          for j, h in enumerate(helpers[p])]
    tr += to_helpers([(X1, S.xin1)], [e for e in on if e not in off])
    g.wait_ge(S.ld2, 32)
    g.remote_dma_fused(tr, local_sem=S.sent)

    g.wait_ge(S.ld3, 32)
    g.remote_dma_fused(to_helpers([(O, S.ovin), (V, S.ovin)], on), local_sem=S.sent)
    g.wait_ge(S.ld4, 32)
    g.remote_dma_fused(to_helpers([(M, S.mwin), (WW, S.mwin)], on), local_sem=S.sent)

    def ystore(q, r):
        q.wait_ge(S["yin%d" % r], 8 * K)
        q.dma_start(T.y[:, F * r:F * r + F], T.yl[K * r:K * r + K]).then_inc(S.st, 16)

    first, second, third = sorted((x0, x1, p), key=lambda k: (cross[k] + plane[k]).index(i))
    g.sync.wait_ge(S.mi, 4 * K)
    g.sync.dma_start(T.mo[:], T.ml[0:K]).then_inc(S.st, 16)
    g.scalar.wait_ge(S.vi, 4 * K)
    g.scalar.dma_start(T.vo[:], T.vl[0:K]).then_inc(S.st, 16)
    ystore(g.scalar, i)
    ystore(g.sync, first)
    ystore(g.scalar, second)
    ystore(g.sync, third)
    g.wait_ge(S.sent, 4 * len(on))
    g.wait_ge(S.st, 96)


def _helper(g, core, T, topo, i, j, cores, helpers, cross, plane):
    S = T.sem
    v = g.vector
    A = AluOpType
    rc = cores[i]
    n_on = len(_bits(topo.mask(rc, core)))
    n_out = len(_bits(topo.mask(cores[plane[i][0]], core)))

    n_off = 0
    for n, k in enumerate(cross[i]):
        dst = helpers[k][j]
        rid, pid = topo.addr(dst, core)
        m = topo.mask(core, dst)
        n_off = len(_bits(m))
        g.wait_ge((S.xin0, S.xin1)[n], (n_on // K, (n_on - n_out) // K)[n])
        g.remote_dma((T.gXa, T.gXb)[n][:], T.hin[(X0, X1)[n]], (S.xa, S.xb)[n], S.fwd, pid, rid, m)

    g.scalar.wait_ge(S.pin, n_out // K)
    g.scalar.dma_start(T.gP[:], T.hin[P]).then_inc(S.lop, 16)
    g.sync.wait_ge(S.ovin, n_on // K)
    g.sync.dma_start(T.gO[:], T.hin[O]).then_inc(S.lop, 16)
    g.sync.dma_start(T.tv[:], T.hin[V]).then_inc(S.lv, 16)
    g.sync.wait_ge(S.mwin, n_on // K)
    g.sync.dma_start(T.tm[:], T.hin[M]).then_inc(S.lm, 16)
    g.sync.dma_start(T.tw[:], T.hin[WW]).then_inc(S.lw, 16)

    pA, pB, pC, pD, pE = (T[n][:, 0:W] for n in ("pA", "pB", "pC", "pD", "pE"))
    done = [0]

    def vop(ins, wait=True):
        ins.then_inc(S.vq, 1)
        done[0] += 1
        if wait:
            v.wait_ge(S.vq, done[0])

    v.wait_ge(S.lv, 16)
    vop(v.tensor_scalar(T.v7[:], T.tv[:], 7.0, None, A.mult), wait=False)
    v.wait_ge(S.lop, 32)
    vop(v.tensor_tensor(pA, T.gO[:], T.gP[:], A.add))
    v.wait_ge(S.xa, n_off)
    vop(v.tensor_tensor(pB, pA, T.gXa[:], A.add))
    v.wait_ge(S.xb, n_off)
    vop(v.tensor_tensor(T.s[:], pB, T.gXb[:], A.add))
    vop(v.tensor_tensor(pC, T.s[:], T.s[:], A.mult))
    vop(v.tensor_tensor(T.v8[:], pC, T.v7[:], A.add))
    g.scalar.wait_ge(S.vq, done[0])
    g.scalar.activation(pD, T.v8[:], ActivationFunctionType.Sqrt, scale=0.5).then_inc(S.sq, 1)
    vop(v.tensor_scalar(T.vo_t[:], T.v8[:], 0.125, None, A.mult), wait=False)
    v.wait_ge(S.lm, 16)
    vop(v.tensor_scalar(pE, T.tm[:], 3.0, None, A.mult))
    vop(v.tensor_tensor(T.u[:], pE, T.s[:], A.add))
    vop(v.tensor_scalar(T.mo_t[:], T.u[:], 0.25, None, A.mult))
    mv_ready = done[0]
    v.wait_ge(S.sq, 1)
    vop(v.tensor_scalar(pD, pD, 2.0 * EPS, None, A.add))
    vop(v.reciprocal(pD, pD))
    vop(v.tensor_tensor(pC, T.u[:], pD, A.mult))
    v.wait_ge(S.lw, 16)
    vop(v.tensor_tensor(T.wn[:], T.tw[:], pC, A.subtract))
    w_ready = done[0]

    peers = [cores[k] for k in cross[i] + plane[i]]
    off = _bits(topo.mask(core, peers[0]))
    for d in peers:
        off = [e for e in off if e in _bits(topo.mask(core, d))]
    rest = [e for e in _bits(topo.mask(core, rc)) if e not in off]
    half = len(rest) // 2

    g.wait_ge(S.vq, mv_ready)
    g.remote_dma_fused([_xfer(topo, core, rc, _mask(rest[:half]), S.mi, T.mo_t[:], T.ml[j]),
                        _xfer(topo, core, rc, _mask(rest[half:]), S.vi, T.vo_t[:], T.vl[j])], local_sem=S.fwd)
    ysem = S["yin%d" % i]
    ids = []
    for d in peers:
        rid, pid = topo.addr(d, core)
        ids.append(DstId(rid=rid, pnc=pid))
    g.wait_ge(S.vq, w_ready)
    g.remote_dma_fused([RemoteDMATransfer(dst_ids=ids, dma_engine_mask=_mask(off), remote_sem=ysem, srcs=[T.wn[:]],
                                          dsts=[T.yl[K * i + j] for _ in peers]),
                        _xfer(topo, core, rc, _mask(rest), ysem, T.wn[:], T.yl[K * i + j])], local_sem=S.fwd)
    g.wait_ge(S.fwd, 2 * n_off + len(off) + 2 * len(rest))


def rank_program(g, core, T, topo):
    cores, helpers, cross, plane = _plan(T, topo)
    rank = T.rank_of(core)
    if rank is not None:
        _rank(g, core, T, topo, rank, helpers, cross, plane)
        return
    for i in range(N):
        if core in helpers[i]:
            _helper(g, core, T, topo, i, helpers[i].index(core), cores, helpers, cross, plane)
